import numpy as np, ml_dtypes
CORES = [83,85,87,115,117,119]
N = 6
BF = ml_dtypes.bfloat16
def f(rng, *shape):
    return (rng.standard_normal(shape, dtype=np.float32) * np.exp2(rng.integers(-2, 3, shape[:-1] + (1,)))).astype(BF)
def wide(rng, *shape):
    v = f(rng, *shape).astype(np.float32); k = shape[:-2] + (1, shape[-1])
    return (v * np.exp2(rng.integers(-6, 7, k)) * (rng.random(k) > 0.0625)).astype(BF)
def gentries(a):
    return np.ascontiguousarray(a.reshape(8, 16, -1).transpose(0, 2, 1)).reshape(8, -1)
def gtable(e):
    e = np.asarray(e); return np.ascontiguousarray(e.reshape(8, -1, 16).transpose(0, 2, 1)).reshape(128, -1).astype(np.int32)
L, K, R, D = 12288, 256, 6, 4095
def corner(rng):
    return rng.integers(0, 4096 - D, (2, 1, 8, 1))
def walk(rng):
    v = np.repeat(rng.integers(-3, 4, (N, 8, L // 64)), 64, axis=2) + rng.integers(-1, 2, (N, 8, L))
    m = (rng.integers(0, D + 1, (N, 8, 1)) + np.add.accumulate(v, axis=2)) % (2 * D)
    return D - np.abs(m - D)
def listeners(rng, o):
    return rng.integers(D, L - 1, (N, 8, K)), o[0] + rng.integers(0, D + 1, (N, 8, K)), o[1] + rng.integers(0, D + 1, (N, 8, K))
def packed(X, Y, s, t, x, z):
    return {"track": (X * 4096 + Y).astype(np.int32), "sound": s, "when": np.stack([gtable(a) for a in t]), "place": np.stack([gtable(a) for a in x * 4096 + z])}
def setup_inputs(rng):
    o = corner(rng); t, x, z = listeners(rng, o)
    return packed(o[0] + walk(rng), o[1] + walk(rng), f(rng, N, 128, L), t, x, z)
def setup_inputs_ends(rng):
    o = np.zeros((2, 1, 8, 1), np.int64); o[:, :, 1::2] = 4095 - D
    X, Y = o[0] + walk(rng), o[1] + walk(rng); t, x, z = listeners(rng, o)
    for g in range(8):
        q = int(rng.integers(0, N)); c = int(o[0, 0, g, 0]); near, far = (c, c + D) if g % 2 == 0 else (c + D, c)
        X[q, g, :D + 1] = near; Y[q, g, :D + 1] = near
        t[:, g, 0] = D; x[:, g, 0] = far; z[:, g, 0] = far
        for r in range(N):
            p = (r + 1) % N; t[r, g, K - 1] = L - 2; x[r, g, K - 1] = X[p, g, L - 2]; z[r, g, K - 1] = Y[p, g, L - 2]
    return packed(X, Y, f(rng, N, 128, L), t, x, z)
def setup_inputs_jumps(rng):
    o = corner(rng); t, x, z = listeners(rng, o)
    return packed(o[0] + rng.integers(0, D + 1, (N, 8, L)), o[1] + rng.integers(0, D + 1, (N, 8, L)), f(rng, N, 128, L), t, x, z)
def setup_inputs_still(rng):
    o = corner(rng); t, x, z = listeners(rng, o); X, Y = o[0] + walk(rng), o[1] + walk(rng)
    q = int(rng.integers(0, N)); r = (q + 1) % N; w = (q + 2) % N
    X[q] = X[q, :, :1].copy(); Y[q] = Y[q, :, :1].copy()
    for a in (t, x, z): a[r, :4] = a[r, :4, :1].copy()
    t[w] = np.sort(t[w], axis=1); x[w] = x[w, :, :1].copy(); z[w] = z[w, :, :1].copy()
    return packed(X, Y, f(rng, N, 128, L), t, x, z)
def setup_inputs_sizes(rng):
    d = np.array([0, 4094, 3, 4000, 64, 3000, 500, 2049]).reshape(1, 8, 1)
    o = rng.integers(0, 4096 - d, (2, 1, 8, 1))
    h = lambda n: rng.integers(0, d + 1, (N, 8, n))
    t = rng.integers(d, L - 1, (N, 8, K)); t[:, 0, 0] = 0
    return packed(o[0] + h(L), o[1] + h(L), f(rng, N, 128, L), t, o[0] + h(K), o[1] + h(K))
def setup_inputs_spread(rng):
    d = setup_inputs(rng); d["sound"] = wide(rng, N, 128, L); return d
def check_inputs(d):
    bad = []; tr = np.asarray(d["track"]).astype(np.int64); pl = np.asarray(d["place"]).astype(np.int64); wh = np.asarray(d["when"]).astype(np.int64)
    if not np.isfinite(np.asarray(d["sound"]).astype(np.float32)).all(): bad.append("finite")
    if tr.min() < 0 or tr.max() >= 4096 * 4096: bad.append("track")
    if pl.min() < 0 or pl.max() >= 4096 * 4096: bad.append("place")
    if wh.min() < 0 or wh.max() > L - 2: bad.append("when")
    ok = True
    for r in range(N):
        t = gentries(wh[r]); w = gentries(pl[r])
        for q in range(N):
            e = np.clip(t, 0, L - 2)
            for i in range(R):
                v = np.take_along_axis(tr[q], e, 1)
                e = t - np.maximum(np.abs((v >> 12) - (w >> 12)), np.abs((v & 4095) - (w & 4095)))
                ok = ok and bool(e.min() >= 0) and bool(e.max() <= L - 2); e = np.clip(e, 0, L - 2)
    if not ok: bad.append("inside")
    return bad
def reference(track, sound, when, place):
    y = np.zeros((N, 128, K), np.float32); s = sound.astype(np.float32).reshape(N, 8, 16, L); tr = track.astype(np.int64)
    for r in range(N):
        t = gentries(when[r]).astype(np.int64); w = gentries(place[r]).astype(np.int64)
        for q in range(N):
            e = t
            for i in range(R):
                v = np.take_along_axis(tr[q], e, 1)
                e = t - np.maximum(np.abs((v >> 12) - (w >> 12)), np.abs((v & 4095) - (w & 4095)))
            u = np.take_along_axis(s[q], e[:, None, :], 2) + np.take_along_axis(s[q], e[:, None, :] + 1, 2)
            y[r] += u.astype(BF).astype(np.float32).reshape(128, K)
    return {"y": y}

@@ -1,0 +1,289 @@
+from concourse.bass import DstId, RemoteDMATransfer
+from concourse.mybir import AluOpType, ActivationFunctionType
+
+L, K, ROUNDS, N = 12288, 256, 6, 6
+H = L // 2
+HC = H // 16
+CA = 16
+FV, FA, FG = 7424, 11136, 11776
+S1 = 4096
+
+SCRATCH = {
+    "win": ("sbuf", [128, L], "bfloat16"),
+    "snd": ("sbuf", [128, L], "bfloat16"),
+    "trk": ("sbuf", [128, 2 * HC], "int32"),
+    "pcs": ("sbuf", [128, 8 * HC], "bfloat16"),
+    "lists": ("sbuf", [128, N, 32], "int32"),
+    "xy": ("sbuf", [128, 192], "int32"),
+    "xd": ("sbuf", [128, 192], "float16"),
+    "yd": ("sbuf", [128, 192], "float16"),
+    "th": ("sbuf", [128, 96], "bfloat16"),
+    "tl": ("sbuf", [128, 96], "bfloat16"),
+    "off": ("sbuf", [128, 96], "uint16"),
+    "off1": ("sbuf", [128, 96], "uint16"),
+    "gat": ("sbuf", [128, 3 * 512], "bfloat16"),
+    "ab": ("sbuf", [128, 3 * 64], "float32"),
+    "cb": ("sbuf", [128, 136 + 128], "bfloat16"),
+    "nb": ("sbuf", [128, 136], "float32"),
+    "rx": ("sbuf", [128, 128], "float16"),
+    "ry": ("sbuf", [128, 128], "float16"),
+    "pcol": ("sbuf", [128, 1], "int32"),
+    "h8": ("sbuf", [128, 1], "int32"),
+    "cols": ("sbuf", [128, 4], "float32"),
+    "s0": ("sbuf", [128, N * K], "bfloat16"),
+    "ub": ("sbuf", [128, N, K], "bfloat16"),
+    "land": ("sbuf", [128, N, K], "bfloat16"),
+    "ya": ("sbuf", [128, 128], "float32"),
+    "yb": ("sbuf", [128, 128], "float32"),
+}
+for _k in range(3):
+    SCRATCH["pr%d" % _k] = ("psum", [128, 512], "float32")
+    SCRATCH["pe%d" % _k] = ("psum", [128, 512], "float32")
+for _k in range(2):
+    SCRATCH["pp%d" % _k] = ("psum", [128, 512], "float32")
+
+SEMAPHORES = ["lin", "sent"] + ["arr%d" % q for q in range(N)] + ["a%d" % i for i in range(120)]
+
+
+def listener_order(r, cores, topo):
+    same = [q for q in range(N) if topo.chip(cores[q]) == topo.chip(cores[r])]
+    far = [q for q in range(N) if q not in same]
+    i = same.index(r)
+    return ([far[(i + j) % len(far)] for j in range(len(far))]
+            + [same[(i + j) % len(same)] for j in range(1, len(same))] + [r])
+
+
+def rank_program(g, core, T, topo):
+    rank = T.rank_of(core)
+    if rank is None:
+        return
+    cores = list(T.cores)
+    order = listener_order(rank, cores, topo)
+    AF, OP = ActivationFunctionType, AluOpType
+    Q = {"g": g, "v": g.vector, "s": g.scalar, "t": g.tensor, "y": g.sync}
+    used = [0]
+    total, seen, best = {}, {}, {}
+
+    def fresh():
+        used[0] += 1
+        return "a%d" % (used[0] - 1)
+
+    def wait(q, deps):
+        for name, val in deps:
+            if seen.get((q, name), 0) < val:
+                Q[q].wait_ge(T.sem[name], val)
+                seen[(q, name)] = val
+                best[name] = max(best.get(name, 0), val)
+
+    def done(ins, name=None, n=1):
+        name = name or fresh()
+        ins.then_inc(T.sem[name], n)
+        total[name] = total.get(name, 0) + n
+        return (name, total[name])
+
+    def bits(engs):
+        return sum(1 << e for e in engs)
+
+    def dst(c):
+        rid, pid, _ = topo.addr(c)
+        return DstId(rid=rid, pnc=pid)
+
+    V, S, PE, Y = g.vector, g.scalar, g.tensor, g.sync
+    me = N - 1
+    far = [q for q in order[:me] if topo.chip(cores[q]) != topo.chip(core)]
+    near = [q for q in order[:me] if q not in far]
+    far_eng = topo.engines(core, cores[far[0]])
+    near_eng = [e for e in topo.engines(core, cores[near[0]]) if e not in far_eng]
+
+    trk_t = [done(Y.dma_start(T.trk[:, h * HC:(h + 1) * HC], T.track[:, h * H:(h + 1) * H]), n=16) for h in range(2)]
+    lw = done(S.dma_start(T.lists[:, me, 0:16], T.when[:]), n=16)
+    lp = done(S.dma_start(T.lists[:, me, 16:32], T.place[:]), n=16)
+    snd1 = done(Y.dma_start(T.snd[:, 0:S1], T.sound[:, 0:S1]), n=16)
+
+    f0 = done(V.memset(T.win[:, 0:512], 0.0))
+    f1 = done(V.memset(T.win[:, 512:2048], 0.0))
+    cz = done(V.memset(T.cb[:], 0.0))
+    f2 = done(V.memset(T.win[:, 2048:FV], 0.0))
+    wait("s", [f0])
+    f3 = done(S.activation(T.win[:, FV:FV + 512], T.win[:, 0:512], AF.Copy))
+    wait("s", [f1])
+    f4 = done(S.activation(T.win[:, FV + 512:FV + 2560], T.win[:, 0:2048], AF.Copy))
+    f5 = done(S.activation(T.win[:, FV + 2560:FA], T.win[:, 0:FA - FV - 2560], AF.Copy))
+    pc = done(g.iota(T.pcol[:], [[0, 1]], 0, 1))
+    nz = done(g.iota(T.nb[:], [[0, 136]], 0, 0, allow_small_or_imprecise_dtypes=True))
+    f6 = done(g.iota(T.win[:, FA:FG], [[0, FG - FA]], 0, 0, allow_small_or_imprecise_dtypes=True))
+
+    wait("g", [lw, lp])
+    g.remote_dma_fused([
+        RemoteDMATransfer(dst_ids=[dst(cores[q]) for q in grp], dma_engine_mask=bits(engs), remote_sem=T.sem.lin,
+                          srcs=[T.lists[:, me, :]],
+                          dsts=[T.lists[:, listener_order(q, cores, topo).index(rank), :] for q in grp])
+        for grp, engs in ((far, far_eng), (near, near_eng))], local_sem=T.sem.sent)
+    total["sent"] = len(far_eng) + len(near_eng)
+    total["lin"] = len(far) * len(far_eng) + len(near) * len(near_eng)
+    lin = ("lin", total["lin"])
+    f7 = done(g.iota(T.win[:, FG:L], [[0, L - FG]], 0, 0, allow_small_or_imprecise_dtypes=True))
+
+    wb, ident = T.cb[:, 0:136], T.cb[:, 136:264]
+    wait("g", [cz, nz])
+    w0 = done(g.affine_select(T.cb[:, 8:136:16], T.cb[:, 8:136:16], [[-16, 8]], OP.is_ge, 0.5, -4, 1))
+    w1 = done(g.affine_select(T.cb[:, 16:136:16], T.cb[:, 16:136:16], [[-16, 8]], OP.is_ge, -0.5, -4, 1))
+    n0 = done(g.affine_select(T.nb[:, 8:136], T.nb[:, 8:136], [[-16, 8], [1000, 2], [-1, 8]], OP.not_equal, -1.0, 0, 1))
+    wait("g", [w0, w1, n0])
+    w2 = done(g.affine_select(T.cb[:, 8:136:8], T.cb[:, 8:136:8], [[-16, 8], [0, 2]], OP.is_ge, 2.0 ** -13, -2, 1))
+    nb_t = done(g.affine_select(T.nb[:, 8:136], T.nb[:, 8:136], [[-16, 8], [1000, 2], [-1, 8]], OP.not_equal, -1.0, -8, 1))
+    wait("g", [w2])
+    wb_t = done(g.affine_select(T.cb[:, 8:136:8], T.cb[:, 8:136:8], [[-16, 8], [0, 2]], OP.is_ge, 0.0, 0, 1))
+    id_t = done(g.affine_select(ident, ident, [[-1, 128]], OP.not_equal, 1.0, 0, 1))
+
+    pp = [T["pp%d" % h][:, 0:HC] for h in range(2)]
+    piece = lambda k, h: T.pcs[:, (2 * k + h) * HC:(2 * k + h + 1) * HC]
+    rem, made = [None, None], {}
+    for h in range(2):
+        wait("v", [trk_t[h]])
+        rem[h] = done(V.tensor_copy(pp[h], T.trk[:, h * HC:(h + 1) * HC]))
+    for k, bias in enumerate((786432.0, -2047.5, 0.0)):
+        for h in range(2):
+            wait("s", [rem[h]])
+            made[(k, h)] = done(S.activation(piece(k, h), pp[h], AF.Identity, bias=bias))
+        for h in range(2):
+            wait("v", [made[(k, h)]])
+            rem[h] = done(V.tensor_tensor(pp[h] if k < 2 else piece(3, h), pp[h], piece(k, h), OP.subtract))
+    for h in range(2):
+        made[(3, h)] = rem[h]
+    laid = fresh()
+    wait("y", [f0, f1, f2, f3, f4, f5, f6])
+    for k in range(4):
+        for h in range(2):
+            if h == 1:
+                wait("y", [f7])
+            wait("y", [made[(k, h)]])
+            win_t = done(Y.dma_start(T.win[k:128:16, h * H:(h + 1) * H], piece(k, h)), laid, 16)
+    wait("y", [win_t])
+    snd2 = done(Y.dma_start(T.snd[:, S1:L], T.sound[:, S1:L]), n=16)
+
+    wait("v", [pc])
+    h8 = done(V.tensor_scalar(T.h8[:], T.pcol[:], 8, None, OP.bitwise_and))
+    wait("v", [nb_t])
+    n_lo, n_hi = T.nb[:, 8:136], T.nb[:, 0:128]
+    rx = done(V.tensor_tensor(T.rx[:], n_lo, n_hi, OP.add))
+    ry = done(V.tensor_tensor(T.ry[:], n_lo, n_hi, OP.subtract))
+    wait("v", [h8])
+    m0 = done(V.tensor_scalar(T.cols[:, 0:1], T.h8[:], -1.0 / 16, 0.5, OP.mult, OP.add))
+    m1 = done(V.tensor_scalar(T.cols[:, 1:2], T.h8[:], 1.0 / 16, None, OP.mult))
+    bu = done(V.tensor_scalar(T.cols[:, 2:3], T.h8[:], 256.0, -2048.0, OP.mult, OP.add))
+    wait("v", [lin, lw, lp])
+    tw, pl = T.lists[:, :, 0:16], T.lists[:, :, 16:32]
+    xi = done(V.tensor_scalar(T.xy[:, 0:96], pl, 12, None, OP.arith_shift_right))
+    yi = done(V.tensor_scalar(T.xy[:, 96:192], pl, 4095, None, OP.bitwise_and))
+    o0 = done(V.tensor_copy(T.off[:], tw))
+    th = done(V.tensor_copy(T.th[:], tw))
+    wait("v", [xi, yi, m0, m1])
+    xyd = []
+    for buf, c0 in ((T.xd, 0), (T.yd, 96)):
+        for h in range(2):
+            xyd.append(done(V.tensor_scalar(buf[:, h:192:2], T.xy[:, c0:c0 + 96], -2048.0, T.cols[:, h:h + 1], OP.add, OP.mult)))
+    wait("v", [th])
+    tl = done(V.tensor_tensor(T.tl[:], tw, T.th[:], OP.subtract))
+
+    NS = 3 * ROUNDS
+    names = {(w, k): fresh() for w in ("ga", "p1", "ab", "p2", "cp") for k in range(3)}
+    ga, p1, ab, p2, cp, cp1 = {}, {}, {}, {}, {}, {}
+    R = lambda s: T["pr%d" % (s % 3)][:, 0:64]
+    E = lambda s: T["pe%d" % (s % 3)][:, 0:32]
+
+    def gather(s):
+        k = s % 3
+        deps = [win_t, o0] if s < 3 else [cp[s - 3]]
+        wait("s", deps)
+        done(S.activation(T.gat[:, 512 * k:512 * k + 16 * CA], T.win[:, 0:L].indirect(T.off[:, 32 * k:32 * k + CA]), AF.Copy), names[("ga", k)])
+        wait("v", deps)
+        ga[s] = done(V.tensor_copy(T.gat[:, 512 * k + 16 * CA:512 * k + 512], T.win[:, 0:L].indirect(T.off[:, 32 * k + CA:32 * k + 32])), names[("ga", k)])
+
+    def forms(s):
+        k = s % 3
+        wait("t", [rx, ry, wb_t] + xyd + rem)
+        PE.matmul(R(s), T.rx[:], T.xd[:, 64 * k:64 * k + 64], True, False)
+        PE.matmul(R(s), T.ry[:], T.yd[:, 64 * k:64 * k + 64], False, False)
+        wait("t", [ga[s]])
+        for a in range(8):
+            ins = PE.matmul(R(s), T.cb[:, 8 - a:136 - a], T.gat[:, 512 * k + a:512 * k + 512:8], False, a == 7)
+        p1[s] = done(ins, names[("p1", k)])
+
+    def absolute(s):
+        k = s % 3
+        wait("s", [p1[s], bu])
+        ab[s] = done(S.activation(T.ab[:, 64 * k:64 * k + 64], R(s), AF.Abs, bias=T.cols[:, 2:3]), names[("ab", k)])
+
+    def emission(s):
+        k = s % 3
+        wait("t", [id_t, nb_t, th, tl])
+        PE.matmul(E(s), ident, T.th[:, 32 * k:32 * k + 32], True, False)
+        PE.matmul(E(s), ident, T.tl[:, 32 * k:32 * k + 32], False, False)
+        wait("t", [ab[s]])
+        PE.matmul(E(s), n_lo, T.ab[:, 64 * k:64 * k + 64:2], False, False)
+        p2[s] = done(PE.matmul(E(s), n_hi, T.ab[:, 64 * k + 1:64 * k + 64:2], False, True), names[("p2", k)])
+
+    def offsets(s):
+        k = s % 3
+        wait("v", [p2[s]])
+        cp[s] = done(V.tensor_copy(T.off[:, 32 * k:32 * k + 32], E(s)), names[("cp", k)])
+        if s >= NS - 3:
+            cp1[k] = done(V.tensor_scalar(T.off1[:, 32 * k:32 * k + 32], E(s), 1.0, None, OP.add))
+
+    for s in range(NS):
+        gather(s)
+        if s >= 2:
+            offsets(s - 2)
+        if s >= 1:
+            absolute(s - 1)
+        forms(s)
+        if s >= 1:
+            emission(s - 1)
+
+    first, u = {}, {}
+
+    def sound_a(i):
+        wait("s", [snd1, snd2, cp[NS - 3 + i // 2]])
+        first[i] = done(S.activation(T.s0[:, K * i:K * (i + 1)], T.snd[:, 0:L].indirect(T.off[:, 16 * i:16 * i + 16]), AF.Copy))
+
+    def sound_b(i):
+        wait("v", [snd1, snd2, first[i], cp1[i // 2]])
+        out = T.land[:, rank, :] if i == me else T.ub[:, i, :]
+        u[i] = done(V.tensor_tensor(out, T.snd[:, 0:L].indirect(T.off1[:, 16 * i:16 * i + 16]), T.s0[:, K * i:K * (i + 1)], OP.add))
+        if i != me:
+            q = order[i]
+            engs = far_eng if q in far else near_eng
+            rid, pid, _ = topo.addr(cores[q])
+            wait("g", [u[i]])
+            g.remote_dma(T.land[:, rank, :], T.ub[:, i, :], T.sem["arr%d" % rank], T.sem.sent, pid, rid, bits(engs))
+            total["sent"] += len(engs)
+
+    sound_a(0)
+    absolute(NS - 1)
+    emission(NS - 1)
+    offsets(NS - 2)
+    sound_b(0)
+    offsets(NS - 1)
+    for i in range(1, N):
+        sound_a(i)
+        sound_b(i)
+
+    for q in range(N):
+        if q == rank:
+            wait("t", [u[me]])
+        else:
+            total["arr%d" % q] = len(far_eng if q in far else near_eng)
+            wait("t", [("arr%d" % q, total["arr%d" % q])])
+        ins0 = PE.matmul(T.pp0[:, 0:128], ident, T.land[:, q, 0:128], q == 0, q == N - 1)
+        ins1 = PE.matmul(T.pp1[:, 0:128], ident, T.land[:, q, 128:256], q == 0, q == N - 1)
+    sa, sb = done(ins0), done(ins1)
+    wait("v", [sa])
+    ya = done(V.tensor_copy(T.ya[:], T.pp0[:, 0:128]))
+    wait("s", [sb])
+    yb = done(S.activation(T.yb[:], T.pp1[:, 0:128], AF.Copy))
+    wait("y", [ya])
+    done(Y.dma_start(T.y[:, 0:128], T.ya[:]), n=16)
+    wait("s", [yb])
+    done(S.dma_start(T.y[:, 128:256], T.yb[:]), n=16)
+    wait("g", [(n, v) for n, v in total.items() if best.get(n, 0) < v])

@@ -4,13 +4,15 @@ from concourse.mybir import AluOpType, ActivationFunctionType
 L, K, ROUNDS, N = 12288, 256, 6, 6
 H = L // 2
 HC = H // 16
-CA = 16
-FV, FA, FG = 7424, 11136, 11776
-S1 = 4096
+CA = 18
+ZW = 768
+FA = L - 8 * ZW
+FV = 3904
 
 SCRATCH = {
     "win": ("sbuf", [128, L], "bfloat16"),
     "snd": ("sbuf", [128, L], "bfloat16"),
+    "zt": ("sbuf", [128, ZW], "bfloat16"),
     "trk": ("sbuf", [128, 2 * HC], "int32"),
     "pcs": ("sbuf", [128, 8 * HC], "bfloat16"),
     "lists": ("sbuf", [128, N, 32], "int32"),
@@ -98,20 +100,28 @@ def rank_program(g, core, T, topo):
     trk_t = [done(Y.dma_start(T.trk[:, h * HC:(h + 1) * HC], T.track[:, h * H:(h + 1) * H]), n=16) for h in range(2)]
     lw = done(S.dma_start(T.lists[:, me, 0:16], T.when[:]), n=16)
     lp = done(S.dma_start(T.lists[:, me, 16:32], T.place[:]), n=16)
-    snd1 = done(Y.dma_start(T.snd[:, 0:S1], T.sound[:, 0:S1]), n=16)
 
-    f0 = done(V.memset(T.win[:, 0:512], 0.0))
-    f1 = done(V.memset(T.win[:, 512:2048], 0.0))
+    f0 = done(V.memset(T.zt[:], 0.0))
     cz = done(V.memset(T.cb[:], 0.0))
-    f2 = done(V.memset(T.win[:, 2048:FV], 0.0))
+    f2 = done(V.memset(T.win[:, 0:FV], 0.0))
+    laid = fresh()
+    wait("y", [f0])
+    for grp in range(8):
+        done(Y.dma_start(T.win[16 * grp + 4:16 * grp + 16, FA:L], T.zt[0:96, :]), laid, 16)
     wait("s", [f0])
-    f3 = done(S.activation(T.win[:, FV:FV + 512], T.win[:, 0:512], AF.Copy))
-    wait("s", [f1])
-    f4 = done(S.activation(T.win[:, FV + 512:FV + 2560], T.win[:, 0:2048], AF.Copy))
-    f5 = done(S.activation(T.win[:, FV + 2560:FA], T.win[:, 0:FA - FV - 2560], AF.Copy))
+    f3 = done(S.activation(T.win[:, FV:FV + ZW], T.zt[:], AF.Copy))
+    f4 = done(S.activation(T.win[:, FV + ZW:FV + 2 * ZW], T.zt[:], AF.Copy))
+    f5 = done(S.activation(T.win[:, FV + 2 * ZW:FA], T.zt[:, 0:FA - FV - 2 * ZW], AF.Copy))
+
+    ident = T.cb[:, 136:264]
     pc = done(g.iota(T.pcol[:], [[0, 1]], 0, 1))
     nz = done(g.iota(T.nb[:], [[0, 136]], 0, 0, allow_small_or_imprecise_dtypes=True))
-    f6 = done(g.iota(T.win[:, FA:FG], [[0, FG - FA]], 0, 0, allow_small_or_imprecise_dtypes=True))
+    wait("g", [cz, nz])
+    n0 = done(g.affine_select(T.nb[:, 8:136], T.nb[:, 8:136], [[-16, 8], [1000, 2], [-1, 8]], OP.not_equal, -1.0, 0, 1))
+    w0 = done(g.affine_select(T.cb[:, 8:136:16], T.cb[:, 8:136:16], [[-16, 8]], OP.is_ge, 0.5, -4, 1))
+    wait("g", [n0])
+    nb_t = done(g.affine_select(T.nb[:, 8:136], T.nb[:, 8:136], [[-16, 8], [1000, 2], [-1, 8]], OP.not_equal, -1.0, -8, 1))
+    w1 = done(g.affine_select(T.cb[:, 16:136:16], T.cb[:, 16:136:16], [[-16, 8]], OP.is_ge, -0.5, -4, 1))
 
     wait("g", [lw, lp])
     g.remote_dma_fused([
@@ -122,19 +132,12 @@ def rank_program(g, core, T, topo):
     total["sent"] = len(far_eng) + len(near_eng)
     total["lin"] = len(far) * len(far_eng) + len(near) * len(near_eng)
     lin = ("lin", total["lin"])
-    f7 = done(g.iota(T.win[:, FG:L], [[0, L - FG]], 0, 0, allow_small_or_imprecise_dtypes=True))
 
-    wb, ident = T.cb[:, 0:136], T.cb[:, 136:264]
-    wait("g", [cz, nz])
-    w0 = done(g.affine_select(T.cb[:, 8:136:16], T.cb[:, 8:136:16], [[-16, 8]], OP.is_ge, 0.5, -4, 1))
-    w1 = done(g.affine_select(T.cb[:, 16:136:16], T.cb[:, 16:136:16], [[-16, 8]], OP.is_ge, -0.5, -4, 1))
-    n0 = done(g.affine_select(T.nb[:, 8:136], T.nb[:, 8:136], [[-16, 8], [1000, 2], [-1, 8]], OP.not_equal, -1.0, 0, 1))
-    wait("g", [w0, w1, n0])
+    wait("g", [w0, w1])
     w2 = done(g.affine_select(T.cb[:, 8:136:8], T.cb[:, 8:136:8], [[-16, 8], [0, 2]], OP.is_ge, 2.0 ** -13, -2, 1))
-    nb_t = done(g.affine_select(T.nb[:, 8:136], T.nb[:, 8:136], [[-16, 8], [1000, 2], [-1, 8]], OP.not_equal, -1.0, -8, 1))
+    id_t = done(g.affine_select(ident, ident, [[-1, 128]], OP.not_equal, 1.0, 0, 1))
     wait("g", [w2])
     wb_t = done(g.affine_select(T.cb[:, 8:136:8], T.cb[:, 8:136:8], [[-16, 8], [0, 2]], OP.is_ge, 0.0, 0, 1))
-    id_t = done(g.affine_select(ident, ident, [[-1, 128]], OP.not_equal, 1.0, 0, 1))
 
     pp = [T["pp%d" % h][:, 0:HC] for h in range(2)]
     piece = lambda k, h: T.pcs[:, (2 * k + h) * HC:(2 * k + h + 1) * HC]
@@ -151,21 +154,18 @@ def rank_program(g, core, T, topo):
             rem[h] = done(V.tensor_tensor(pp[h] if k < 2 else piece(3, h), pp[h], piece(k, h), OP.subtract))
     for h in range(2):
         made[(3, h)] = rem[h]
-    laid = fresh()
-    wait("y", [f0, f1, f2, f3, f4, f5, f6])
+    wait("y", [f2, f3, f4, f5])
     for k in range(4):
         for h in range(2):
-            if h == 1:
-                wait("y", [f7])
             wait("y", [made[(k, h)]])
             win_t = done(Y.dma_start(T.win[k:128:16, h * H:(h + 1) * H], piece(k, h)), laid, 16)
-    wait("y", [win_t])
-    snd2 = done(Y.dma_start(T.snd[:, S1:L], T.sound[:, S1:L]), n=16)
+    snd_t = done(Y.dma_start(T.snd[:], T.sound[:]), n=16)
 
+    tw, pl = T.lists[:, :, 0:16], T.lists[:, :, 16:32]
+    n_lo, n_hi = T.nb[:, 8:136], T.nb[:, 0:128]
     wait("v", [pc])
     h8 = done(V.tensor_scalar(T.h8[:], T.pcol[:], 8, None, OP.bitwise_and))
     wait("v", [nb_t])
-    n_lo, n_hi = T.nb[:, 8:136], T.nb[:, 0:128]
     rx = done(V.tensor_tensor(T.rx[:], n_lo, n_hi, OP.add))
     ry = done(V.tensor_tensor(T.ry[:], n_lo, n_hi, OP.subtract))
     wait("v", [h8])
@@ -173,10 +173,9 @@ def rank_program(g, core, T, topo):
     m1 = done(V.tensor_scalar(T.cols[:, 1:2], T.h8[:], 1.0 / 16, None, OP.mult))
     bu = done(V.tensor_scalar(T.cols[:, 2:3], T.h8[:], 256.0, -2048.0, OP.mult, OP.add))
     wait("v", [lin, lw, lp])
-    tw, pl = T.lists[:, :, 0:16], T.lists[:, :, 16:32]
+    o0 = done(V.tensor_copy(T.off[:], tw))
     xi = done(V.tensor_scalar(T.xy[:, 0:96], pl, 12, None, OP.arith_shift_right))
     yi = done(V.tensor_scalar(T.xy[:, 96:192], pl, 4095, None, OP.bitwise_and))
-    o0 = done(V.tensor_copy(T.off[:], tw))
     th = done(V.tensor_copy(T.th[:], tw))
     wait("v", [xi, yi, m0, m1])
     xyd = []
@@ -200,11 +199,19 @@ def rank_program(g, core, T, topo):
         wait("v", deps)
         ga[s] = done(V.tensor_copy(T.gat[:, 512 * k + 16 * CA:512 * k + 512], T.win[:, 0:L].indirect(T.off[:, 32 * k + CA:32 * k + 32])), names[("ga", k)])
 
+    def times(s):
+        k = s % 3
+        wait("t", [id_t, nb_t, th, tl])
+        PE.matmul(E(s), ident, T.th[:, 32 * k:32 * k + 32], True, False)
+        PE.matmul(E(s), ident, T.tl[:, 32 * k:32 * k + 32], False, False)
+
     def forms(s):
         k = s % 3
         wait("t", [rx, ry, wb_t] + xyd + rem)
         PE.matmul(R(s), T.rx[:], T.xd[:, 64 * k:64 * k + 64], True, False)
         PE.matmul(R(s), T.ry[:], T.yd[:, 64 * k:64 * k + 64], False, False)
+        if s > 0:
+            times(s - 1)
         wait("t", [ga[s]])
         for a in range(8):
             ins = PE.matmul(R(s), T.cb[:, 8 - a:136 - a], T.gat[:, 512 * k + a:512 * k + 512:8], False, a == 7)
@@ -217,9 +224,6 @@ def rank_program(g, core, T, topo):
 
     def emission(s):
         k = s % 3
-        wait("t", [id_t, nb_t, th, tl])
-        PE.matmul(E(s), ident, T.th[:, 32 * k:32 * k + 32], True, False)
-        PE.matmul(E(s), ident, T.tl[:, 32 * k:32 * k + 32], False, False)
         wait("t", [ab[s]])
         PE.matmul(E(s), n_lo, T.ab[:, 64 * k:64 * k + 64:2], False, False)
         p2[s] = done(PE.matmul(E(s), n_hi, T.ab[:, 64 * k + 1:64 * k + 64:2], False, True), names[("p2", k)])
@@ -243,12 +247,13 @@ def rank_program(g, core, T, topo):
 
     first, u = {}, {}
 
-    def sound_a(i):
-        wait("s", [snd1, snd2, cp[NS - 3 + i // 2]])
-        first[i] = done(S.activation(T.s0[:, K * i:K * (i + 1)], T.snd[:, 0:L].indirect(T.off[:, 16 * i:16 * i + 16]), AF.Copy))
+    def sound_a(i, q="s", c0=0, c1=16):
+        wait(q, [snd_t, cp[NS - 3 + i // 2]])
+        out, src = T.s0[:, K * i + 16 * c0:K * i + 16 * c1], T.snd[:, 0:L].indirect(T.off[:, 16 * i + c0:16 * i + c1])
+        first.setdefault(i, []).append(done(S.activation(out, src, AF.Copy) if q == "s" else V.tensor_copy(out, src)))
 
     def sound_b(i):
-        wait("v", [snd1, snd2, first[i], cp1[i // 2]])
+        wait("v", [snd_t, cp1[i // 2]] + first[i])
         out = T.land[:, rank, :] if i == me else T.ub[:, i, :]
         u[i] = done(V.tensor_tensor(out, T.snd[:, 0:L].indirect(T.off1[:, 16 * i:16 * i + 16]), T.s0[:, K * i:K * (i + 1)], OP.add))
         if i != me:
@@ -259,14 +264,18 @@ def rank_program(g, core, T, topo):
             g.remote_dma(T.land[:, rank, :], T.ub[:, i, :], T.sem["arr%d" % rank], T.sem.sent, pid, rid, bits(engs))
             total["sent"] += len(engs)
 
-    sound_a(0)
+    times(NS - 1)
+    sound_a(0, "s", 0, 10)
+    sound_a(0, "v", 10, 16)
     absolute(NS - 1)
     emission(NS - 1)
     offsets(NS - 2)
+    sound_a(1)
     sound_b(0)
     offsets(NS - 1)
     for i in range(1, N):
-        sound_a(i)
+        if i + 1 < N:
+            sound_a(i + 1)
         sound_b(i)
 
     for q in range(N):

@@ -4,39 +4,40 @@ from concourse.mybir import AluOpType, ActivationFunctionType
 L, K, ROUNDS, N = 12288, 256, 6, 6
 H = L // 2
 HC = H // 16
-CA = 18
-ZW = 768
-FA = L - 8 * ZW
-FV = 3904
+QC = HC // 2
+CA = 16
+Z0, ZW = 256, 704
+FV, FG, FA = 3584, 4480, 6144
+YA = 128
+LAG = (0.0, 0.3, 0.6, 0.9)
 
 SCRATCH = {
     "win": ("sbuf", [128, L], "bfloat16"),
     "snd": ("sbuf", [128, L], "bfloat16"),
-    "zt": ("sbuf", [128, ZW], "bfloat16"),
     "trk": ("sbuf", [128, 2 * HC], "int32"),
     "pcs": ("sbuf", [128, 8 * HC], "bfloat16"),
     "lists": ("sbuf", [128, N, 32], "int32"),
     "xy": ("sbuf", [128, 192], "int32"),
+    "xf": ("sbuf", [128, 192], "float16"),
     "xd": ("sbuf", [128, 192], "float16"),
-    "yd": ("sbuf", [128, 192], "float16"),
-    "th": ("sbuf", [128, 96], "bfloat16"),
-    "tl": ("sbuf", [128, 96], "bfloat16"),
+    "tt": ("sbuf", [128, 192], "bfloat16"),
     "off": ("sbuf", [128, 96], "uint16"),
     "off1": ("sbuf", [128, 96], "uint16"),
     "gat": ("sbuf", [128, 3 * 512], "bfloat16"),
     "ab": ("sbuf", [128, 3 * 64], "float32"),
     "cb": ("sbuf", [128, 136 + 128], "bfloat16"),
     "nb": ("sbuf", [128, 136], "float32"),
-    "rx": ("sbuf", [128, 128], "float16"),
-    "ry": ("sbuf", [128, 128], "float16"),
+    "sh": ("sbuf", [128, 2, 136], "bfloat16"),
+    "rt": ("sbuf", [128, 128], "float32"),
+    "rot": ("sbuf", [128, 128], "bfloat16"),
     "pcol": ("sbuf", [128, 1], "int32"),
     "h8": ("sbuf", [128, 1], "int32"),
     "cols": ("sbuf", [128, 4], "float32"),
     "s0": ("sbuf", [128, N * K], "bfloat16"),
     "ub": ("sbuf", [128, N, K], "bfloat16"),
     "land": ("sbuf", [128, N, K], "bfloat16"),
-    "ya": ("sbuf", [128, 128], "float32"),
-    "yb": ("sbuf", [128, 128], "float32"),
+    "ya": ("sbuf", [128, YA], "float32"),
+    "yb": ("sbuf", [128, K - YA], "float32"),
 }
 for _k in range(3):
     SCRATCH["pr%d" % _k] = ("psum", [128, 512], "float32")
@@ -44,7 +45,7 @@ for _k in range(3):
 for _k in range(2):
     SCRATCH["pp%d" % _k] = ("psum", [128, 512], "float32")
 
-SEMAPHORES = ["lin", "sent"] + ["arr%d" % q for q in range(N)] + ["a%d" % i for i in range(120)]
+SEMAPHORES = ["lin", "sent"] + ["arr%d" % q for q in range(N)] + ["a%d" % i for i in range(140)]
 
 
 def listener_order(r, cores, topo):
@@ -97,31 +98,27 @@ def rank_program(g, core, T, topo):
     far_eng = topo.engines(core, cores[far[0]])
     near_eng = [e for e in topo.engines(core, cores[near[0]]) if e not in far_eng]
 
-    trk_t = [done(Y.dma_start(T.trk[:, h * HC:(h + 1) * HC], T.track[:, h * H:(h + 1) * H]), n=16) for h in range(2)]
+    def tile_engines(src, to):
+        every = topo.engines(cores[src], cores[to])
+        last = listener_order(src, cores, topo)[me - 1] == to
+        return every if last or len(every) == len(far_eng) else near_eng
+
     lw = done(S.dma_start(T.lists[:, me, 0:16], T.when[:]), n=16)
-    lp = done(S.dma_start(T.lists[:, me, 16:32], T.place[:]), n=16)
-
-    f0 = done(V.memset(T.zt[:], 0.0))
-    cz = done(V.memset(T.cb[:], 0.0))
-    f2 = done(V.memset(T.win[:, 0:FV], 0.0))
+    lp = done(Y.dma_start(T.lists[:, me, 16:32], T.place[:]), n=16)
+    trk_t = [done(Y.dma_start(T.trk[:, h * HC:(h + 1) * HC], T.track[:, h * H:(h + 1) * H]), n=16) for h in range(2)]
     laid = fresh()
-    wait("y", [f0])
     for grp in range(8):
-        done(Y.dma_start(T.win[16 * grp + 4:16 * grp + 16, FA:L], T.zt[0:96, :]), laid, 16)
+        rows = slice(16 * grp + 4, 16 * grp + 16)
+        done(Y.dma_start(T.win[rows, FA:L], T.sound[rows, FA:L]), laid, 16)
+    f0 = done(V.memset(T.win[:, 0:Z0], 0.0))
+    f1 = done(V.memset(T.win[:, Z0:ZW], 0.0))
+    fv = done(V.memset(T.win[:, ZW:FV], 0.0))
+    cz = done(V.memset(T.cb[:], 0.0))
     wait("s", [f0])
-    f3 = done(S.activation(T.win[:, FV:FV + ZW], T.zt[:], AF.Copy))
-    f4 = done(S.activation(T.win[:, FV + ZW:FV + 2 * ZW], T.zt[:], AF.Copy))
-    f5 = done(S.activation(T.win[:, FV + 2 * ZW:FA], T.zt[:, 0:FA - FV - 2 * ZW], AF.Copy))
-
-    ident = T.cb[:, 136:264]
-    pc = done(g.iota(T.pcol[:], [[0, 1]], 0, 1))
-    nz = done(g.iota(T.nb[:], [[0, 136]], 0, 0, allow_small_or_imprecise_dtypes=True))
-    wait("g", [cz, nz])
-    n0 = done(g.affine_select(T.nb[:, 8:136], T.nb[:, 8:136], [[-16, 8], [1000, 2], [-1, 8]], OP.not_equal, -1.0, 0, 1))
-    w0 = done(g.affine_select(T.cb[:, 8:136:16], T.cb[:, 8:136:16], [[-16, 8]], OP.is_ge, 0.5, -4, 1))
-    wait("g", [n0])
-    nb_t = done(g.affine_select(T.nb[:, 8:136], T.nb[:, 8:136], [[-16, 8], [1000, 2], [-1, 8]], OP.not_equal, -1.0, -8, 1))
-    w1 = done(g.affine_select(T.cb[:, 16:136:16], T.cb[:, 16:136:16], [[-16, 8]], OP.is_ge, -0.5, -4, 1))
+    fs = [done(S.activation(T.win[:, FG:FG + Z0], T.win[:, 0:Z0], AF.Copy))]
+    wait("s", [f1])
+    fs += [done(S.activation(T.win[:, c:min(c + ZW, FA)], T.win[:, 0:min(ZW, FA - c)], AF.Copy)) for c in range(FG + Z0, FA, ZW)]
+    fs.append(done(g.iota(T.win[:, FV:FG], [[0, FG - FV]], 0, 0, allow_small_or_imprecise_dtypes=True)))
 
     wait("g", [lw, lp])
     g.remote_dma_fused([
@@ -133,63 +130,88 @@ def rank_program(g, core, T, topo):
     total["lin"] = len(far) * len(far_eng) + len(near) * len(near_eng)
     lin = ("lin", total["lin"])
 
+    ident = T.cb[:, 136:264]
+    nz = done(g.iota(T.nb[:], [[0, 136]], 0, 0, allow_small_or_imprecise_dtypes=True))
+    pc = done(g.iota(T.pcol[:], [[0, 1]], 0, 1))
+    wait("g", [nz, cz])
+    n0 = done(g.affine_select(T.nb[:, 8:136], T.nb[:, 8:136], [[-16, 8], [1000, 2], [-1, 8]], OP.not_equal, -1.0, 0, 1))
+    w0 = done(g.affine_select(T.cb[:, 8:136:16], T.cb[:, 8:136:16], [[-16, 8]], OP.is_ge, 0.5, -4, 1))
+    w1 = done(g.affine_select(T.cb[:, 16:136:16], T.cb[:, 16:136:16], [[-16, 8]], OP.is_ge, -0.5, -4, 1))
+    wait("g", [n0])
+    nb_t = done(g.affine_select(T.nb[:, 8:136], T.nb[:, 8:136], [[-16, 8], [1000, 2], [-1, 8]], OP.not_equal, -1.0, -8, 1))
     wait("g", [w0, w1])
     w2 = done(g.affine_select(T.cb[:, 8:136:8], T.cb[:, 8:136:8], [[-16, 8], [0, 2]], OP.is_ge, 2.0 ** -13, -2, 1))
     id_t = done(g.affine_select(ident, ident, [[-1, 128]], OP.not_equal, 1.0, 0, 1))
     wait("g", [w2])
     wb_t = done(g.affine_select(T.cb[:, 8:136:8], T.cb[:, 8:136:8], [[-16, 8], [0, 2]], OP.is_ge, 0.0, 0, 1))
 
-    pp = [T["pp%d" % h][:, 0:HC] for h in range(2)]
-    piece = lambda k, h: T.pcs[:, (2 * k + h) * HC:(2 * k + h + 1) * HC]
-    rem, made = [None, None], {}
-    for h in range(2):
-        wait("v", [trk_t[h]])
-        rem[h] = done(V.tensor_copy(pp[h], T.trk[:, h * HC:(h + 1) * HC]))
-    for k, bias in enumerate((786432.0, -2047.5, 0.0)):
-        for h in range(2):
-            wait("s", [rem[h]])
-            made[(k, h)] = done(S.activation(piece(k, h), pp[h], AF.Identity, bias=bias))
-        for h in range(2):
-            wait("v", [made[(k, h)]])
-            rem[h] = done(V.tensor_tensor(pp[h] if k < 2 else piece(3, h), pp[h], piece(k, h), OP.subtract))
-    for h in range(2):
-        made[(3, h)] = rem[h]
-    wait("y", [f2, f3, f4, f5])
-    for k in range(4):
-        for h in range(2):
-            wait("y", [made[(k, h)]])
-            win_t = done(Y.dma_start(T.win[k:128:16, h * H:(h + 1) * H], piece(k, h)), laid, 16)
+    pp = [b[:, 0:QC] for b in (T.pp0, T.pp1, T.pr2, T.pe2)]
+    piece = lambda k, c: T.pcs[:, (4 * k + c) * QC:(4 * k + c + 1) * QC]
+    bias = (786432.0, -2047.5, 0.0)
+    rem, made = {}, {}
+    wait("y", [fv] + fs)
+    for _, k, c in sorted((k + LAG[c], k, c) for k in range(4) for c in range(4)):
+        if k == 0:
+            wait("v", [trk_t[c // 2]])
+            rem[c] = done(V.tensor_copy(pp[c], T.trk[:, c * QC:(c + 1) * QC]))
+        else:
+            wait("v", [made[(k - 1, c)]])
+            rem[c] = done(V.tensor_tensor(pp[c] if k < 3 else piece(3, c), pp[c], piece(k - 1, c), OP.subtract))
+        if k < 3:
+            wait("s", [rem[c]])
+            made[(k, c)] = done(S.activation(piece(k, c), pp[c], AF.Identity, bias=bias[k]))
+        else:
+            made[(k, c)] = rem[c]
+        if c % 2 == 1:
+            h = c // 2
+            wait("y", [made[(k, c - 1)], made[(k, c)]])
+            win_t = done(Y.dma_start(T.win[k:128:16, h * H:(h + 1) * H], T.pcs[:, (2 * k + h) * HC:(2 * k + h + 1) * HC]), laid, 16)
     snd_t = done(Y.dma_start(T.snd[:], T.sound[:]), n=16)
+    banks_free = [made[(3, c)] for c in range(4)]
 
     tw, pl = T.lists[:, :, 0:16], T.lists[:, :, 16:32]
     n_lo, n_hi = T.nb[:, 8:136], T.nb[:, 0:128]
     wait("v", [pc])
     h8 = done(V.tensor_scalar(T.h8[:], T.pcol[:], 8, None, OP.bitwise_and))
-    wait("v", [nb_t])
-    rx = done(V.tensor_tensor(T.rx[:], n_lo, n_hi, OP.add))
-    ry = done(V.tensor_tensor(T.ry[:], n_lo, n_hi, OP.subtract))
     wait("v", [h8])
-    m0 = done(V.tensor_scalar(T.cols[:, 0:1], T.h8[:], -1.0 / 16, 0.5, OP.mult, OP.add))
-    m1 = done(V.tensor_scalar(T.cols[:, 1:2], T.h8[:], 1.0 / 16, None, OP.mult))
+    m0 = done(V.tensor_scalar(T.cols[:, 0:1], T.h8[:], 1.0 / 8, -1.0, OP.mult, OP.add))
+    m1 = done(V.tensor_scalar(T.cols[:, 1:2], T.h8[:], -1.0 / 8, None, OP.mult))
+    sg = done(V.tensor_scalar(T.cols[:, 3:4], T.h8[:], -0.25, 1.0, OP.mult, OP.add))
     bu = done(V.tensor_scalar(T.cols[:, 2:3], T.h8[:], 256.0, -2048.0, OP.mult, OP.add))
+    wait("s", [nb_t, m0, m1])
+    sh = [done(S.activation(T.sh[:, h, :], T.nb[:], AF.Identity, scale=T.cols[:, h:h + 1])) for h in range(2)]
+    wait("s", [sg])
+    rt = done(S.activation(T.rt[:], n_hi, AF.Identity, scale=T.cols[:, 3:4]))
     wait("v", [lin, lw, lp])
-    o0 = done(V.tensor_copy(T.off[:], tw))
     xi = done(V.tensor_scalar(T.xy[:, 0:96], pl, 12, None, OP.arith_shift_right))
     yi = done(V.tensor_scalar(T.xy[:, 96:192], pl, 4095, None, OP.bitwise_and))
-    th = done(V.tensor_copy(T.th[:], tw))
-    wait("v", [xi, yi, m0, m1])
-    xyd = []
-    for buf, c0 in ((T.xd, 0), (T.yd, 96)):
-        for h in range(2):
-            xyd.append(done(V.tensor_scalar(buf[:, h:192:2], T.xy[:, c0:c0 + 96], -2048.0, T.cols[:, h:h + 1], OP.add, OP.mult)))
+    o0 = done(V.tensor_copy(T.off[:], tw))
+    th = done(V.tensor_copy(T.tt[:, 0:96], tw))
+    wait("v", [xi, yi])
+    xf = done(V.tensor_scalar(T.xf[:], T.xy[:], -2048.0, 0.5, OP.add, OP.mult))
     wait("v", [th])
-    tl = done(V.tensor_tensor(T.tl[:], tw, T.th[:], OP.subtract))
+    tl = done(V.tensor_tensor(T.tt[:, 96:192], tw, T.tt[:, 0:96], OP.subtract))
+    wait("v", [nb_t, rt])
+    rot = done(V.tensor_tensor(T.rot[:], n_lo, T.rt[:], OP.add))
+    wait("t", sh + [xf] + banks_free)
+    for h in range(2):
+        for c in range(2):
+            ins = PE.matmul(T.pp0[:, h:192:2], T.sh[:, h, 8 - 8 * c:136 - 8 * c], T.xf[:, 96 * c:96 * c + 96], h + c == 0, h + c == 2)
+    xp = done(ins)
+    wait("v", [xp])
+    xd = done(V.tensor_copy(T.xd[:], T.pp0[:, 0:192]))
 
     NS = 3 * ROUNDS
     names = {(w, k): fresh() for w in ("ga", "p1", "ab", "p2", "cp") for k in range(3)}
     ga, p1, ab, p2, cp, cp1 = {}, {}, {}, {}, {}, {}
     R = lambda s: T["pr%d" % (s % 3)][:, 0:64]
     E = lambda s: T["pe%d" % (s % 3)][:, 0:32]
+
+    def times(s):
+        k = s % 3
+        wait("t", [id_t, th, tl])
+        for c in range(2):
+            PE.matmul(E(s), ident, T.tt[:, 96 * c + 32 * k:96 * c + 32 * k + 32], c == 0, False)
 
     def gather(s):
         k = s % 3
@@ -199,20 +221,13 @@ def rank_program(g, core, T, topo):
         wait("v", deps)
         ga[s] = done(V.tensor_copy(T.gat[:, 512 * k + 16 * CA:512 * k + 512], T.win[:, 0:L].indirect(T.off[:, 32 * k + CA:32 * k + 32])), names[("ga", k)])
 
-    def times(s):
-        k = s % 3
-        wait("t", [id_t, nb_t, th, tl])
-        PE.matmul(E(s), ident, T.th[:, 32 * k:32 * k + 32], True, False)
-        PE.matmul(E(s), ident, T.tl[:, 32 * k:32 * k + 32], False, False)
-
     def forms(s):
         k = s % 3
-        wait("t", [rx, ry, wb_t] + xyd + rem)
-        PE.matmul(R(s), T.rx[:], T.xd[:, 64 * k:64 * k + 64], True, False)
-        PE.matmul(R(s), T.ry[:], T.yd[:, 64 * k:64 * k + 64], False, False)
+        wait("t", [rot, xd])
+        PE.matmul(R(s), T.rot[:], T.xd[:, 64 * k:64 * k + 64], True, False)
         if s > 0:
             times(s - 1)
-        wait("t", [ga[s]])
+        wait("t", [wb_t, ga[s]])
         for a in range(8):
             ins = PE.matmul(R(s), T.cb[:, 8 - a:136 - a], T.gat[:, 512 * k + a:512 * k + 512:8], False, a == 7)
         p1[s] = done(ins, names[("p1", k)])
@@ -258,41 +273,48 @@ def rank_program(g, core, T, topo):
         u[i] = done(V.tensor_tensor(out, T.snd[:, 0:L].indirect(T.off1[:, 16 * i:16 * i + 16]), T.s0[:, K * i:K * (i + 1)], OP.add))
         if i != me:
             q = order[i]
-            engs = far_eng if q in far else near_eng
+            engs = tile_engines(rank, q)
             rid, pid, _ = topo.addr(cores[q])
             wait("g", [u[i]])
             g.remote_dma(T.land[:, rank, :], T.ub[:, i, :], T.sem["arr%d" % rank], T.sem.sent, pid, rid, bits(engs))
             total["sent"] += len(engs)
 
     times(NS - 1)
-    sound_a(0, "s", 0, 10)
-    sound_a(0, "v", 10, 16)
+    sound_a(0, "s", 0, 8)
+    sound_a(0, "v", 8, 16)
     absolute(NS - 1)
     emission(NS - 1)
-    offsets(NS - 2)
     sound_a(1)
     sound_b(0)
+    offsets(NS - 2)
+    sound_a(2)
+    sound_b(1)
     offsets(NS - 1)
-    for i in range(1, N):
+    for i in range(2, N):
         if i + 1 < N:
             sound_a(i + 1)
         sound_b(i)
 
-    for q in range(N):
+    late = [q for q in near if listener_order(q, cores, topo)[me - 1] == rank][0]
+    cut = min(late, rank)
+    parts = ((T.pp0, 0, YA), (T.pp1, YA, K))
+    ends = {}
+    wait("t", [xd])
+    for q, p in [(q, p) for q in range(cut) for p in range(2)] + [(q, p) for p in range(2) for q in range(cut, N)]:
         if q == rank:
             wait("t", [u[me]])
         else:
-            total["arr%d" % q] = len(far_eng if q in far else near_eng)
+            total["arr%d" % q] = len(tile_engines(q, rank))
             wait("t", [("arr%d" % q, total["arr%d" % q])])
-        ins0 = PE.matmul(T.pp0[:, 0:128], ident, T.land[:, q, 0:128], q == 0, q == N - 1)
-        ins1 = PE.matmul(T.pp1[:, 0:128], ident, T.land[:, q, 128:256], q == 0, q == N - 1)
-    sa, sb = done(ins0), done(ins1)
-    wait("v", [sa])
-    ya = done(V.tensor_copy(T.ya[:], T.pp0[:, 0:128]))
-    wait("s", [sb])
-    yb = done(S.activation(T.yb[:], T.pp1[:, 0:128], AF.Copy))
-    wait("y", [ya])
-    done(Y.dma_start(T.y[:, 0:128], T.ya[:]), n=16)
-    wait("s", [yb])
-    done(S.dma_start(T.y[:, 128:256], T.yb[:]), n=16)
+        bank, c0, c1 = parts[p]
+        ends[p] = PE.matmul(bank[:, 0:c1 - c0], ident, T.land[:, q, c0:c1], q == 0, q == N - 1)
+    sa, sb = done(ends[0]), done(ends[1])
+    wait("s", [sa])
+    ya = done(S.activation(T.ya[:], T.pp0[:, 0:YA], AF.Copy))
+    wait("v", [sb])
+    yb = done(V.tensor_copy(T.yb[:], T.pp1[:, 0:K - YA]))
+    wait("s", [ya])
+    done(S.dma_start(T.y[:, 0:YA], T.ya[:]), n=16)
+    wait("y", [yb])
+    done(Y.dma_start(T.y[:, YA:K], T.yb[:]), n=16)
     wait("g", [(n, v) for n, v in total.items() if best.get(n, 0) < v])

from concourse.bass import DstId, RemoteDMATransfer
from concourse.mybir import AluOpType, ActivationFunctionType

L, K, ROUNDS, N = 12288, 256, 6, 6
H = L // 2
HC = H // 16
QC = HC // 2
CA = 16
Z0, ZW = 256, 704
FV, FG, FA = 3584, 4480, 6144
YA = 128
LAG = (0.0, 0.3, 0.6, 0.9)

SCRATCH = {
    "win": ("sbuf", [128, L], "bfloat16"),
    "snd": ("sbuf", [128, L], "bfloat16"),
    "trk": ("sbuf", [128, 2 * HC], "int32"),
    "pcs": ("sbuf", [128, 8 * HC], "bfloat16"),
    "lists": ("sbuf", [128, N, 32], "int32"),
    "xy": ("sbuf", [128, 192], "int32"),
    "xf": ("sbuf", [128, 192], "float16"),
    "xd": ("sbuf", [128, 192], "float16"),
    "tt": ("sbuf", [128, 192], "bfloat16"),
    "off": ("sbuf", [128, 96], "uint16"),
    "off1": ("sbuf", [128, 96], "uint16"),
    "gat": ("sbuf", [128, 3 * 512], "bfloat16"),
    "ab": ("sbuf", [128, 3 * 64], "float32"),
    "cb": ("sbuf", [128, 136 + 128], "bfloat16"),
    "nb": ("sbuf", [128, 136], "float32"),
    "sh": ("sbuf", [128, 2, 136], "bfloat16"),
    "rt": ("sbuf", [128, 128], "float32"),
    "rot": ("sbuf", [128, 128], "bfloat16"),
    "pcol": ("sbuf", [128, 1], "int32"),
    "h8": ("sbuf", [128, 1], "int32"),
    "cols": ("sbuf", [128, 4], "float32"),
    "s0": ("sbuf", [128, N * K], "bfloat16"),
    "ub": ("sbuf", [128, N, K], "bfloat16"),
    "land": ("sbuf", [128, N, K], "bfloat16"),
    "ya": ("sbuf", [128, YA], "float32"),
    "yb": ("sbuf", [128, K - YA], "float32"),
}
for _k in range(3):
    SCRATCH["pr%d" % _k] = ("psum", [128, 512], "float32")
    SCRATCH["pe%d" % _k] = ("psum", [128, 512], "float32")
for _k in range(2):
    SCRATCH["pp%d" % _k] = ("psum", [128, 512], "float32")

SEMAPHORES = ["lin", "sent"] + ["arr%d" % q for q in range(N)] + ["a%d" % i for i in range(140)]


def listener_order(r, cores, topo):
    same = [q for q in range(N) if topo.chip(cores[q]) == topo.chip(cores[r])]
    far = [q for q in range(N) if q not in same]
    i = same.index(r)
    return ([far[(i + j) % len(far)] for j in range(len(far))]
            + [same[(i + j) % len(same)] for j in range(1, len(same))] + [r])


def rank_program(g, core, T, topo):
    rank = T.rank_of(core)
    if rank is None:
        return
    cores = list(T.cores)
    order = listener_order(rank, cores, topo)
    AF, OP = ActivationFunctionType, AluOpType
    Q = {"g": g, "v": g.vector, "s": g.scalar, "t": g.tensor, "y": g.sync}
    used = [0]
    total, seen, best = {}, {}, {}

    def fresh():
        used[0] += 1
        return "a%d" % (used[0] - 1)

    def wait(q, deps):
        for name, val in deps:
            if seen.get((q, name), 0) < val:
                Q[q].wait_ge(T.sem[name], val)
                seen[(q, name)] = val
                best[name] = max(best.get(name, 0), val)

    def done(ins, name=None, n=1):
        name = name or fresh()
        ins.then_inc(T.sem[name], n)
        total[name] = total.get(name, 0) + n
        return (name, total[name])

    def bits(engs):
        return sum(1 << e for e in engs)

    def dst(c):
        rid, pid, _ = topo.addr(c)
        return DstId(rid=rid, pnc=pid)

    V, S, PE, Y = g.vector, g.scalar, g.tensor, g.sync
    me = N - 1
    far = [q for q in order[:me] if topo.chip(cores[q]) != topo.chip(core)]
    near = [q for q in order[:me] if q not in far]
    far_eng = topo.engines(core, cores[far[0]])
    near_eng = [e for e in topo.engines(core, cores[near[0]]) if e not in far_eng]

    def tile_engines(src, to):
        every = topo.engines(cores[src], cores[to])
        last = listener_order(src, cores, topo)[me - 1] == to
        return every if last or len(every) == len(far_eng) else near_eng

    lw = done(S.dma_start(T.lists[:, me, 0:16], T.when[:]), n=16)
    lp = done(Y.dma_start(T.lists[:, me, 16:32], T.place[:]), n=16)
    trk_t = [done(Y.dma_start(T.trk[:, h * HC:(h + 1) * HC], T.track[:, h * H:(h + 1) * H]), n=16) for h in range(2)]
    laid = fresh()
    for grp in range(8):
        rows = slice(16 * grp + 4, 16 * grp + 16)
        done(Y.dma_start(T.win[rows, FA:L], T.sound[rows, FA:L]), laid, 16)
    f0 = done(V.memset(T.win[:, 0:Z0], 0.0))
    f1 = done(V.memset(T.win[:, Z0:ZW], 0.0))
    fv = done(V.memset(T.win[:, ZW:FV], 0.0))
    cz = done(V.memset(T.cb[:], 0.0))
    wait("s", [f0])
    fs = [done(S.activation(T.win[:, FG:FG + Z0], T.win[:, 0:Z0], AF.Copy))]
    wait("s", [f1])
    fs += [done(S.activation(T.win[:, c:min(c + ZW, FA)], T.win[:, 0:min(ZW, FA - c)], AF.Copy)) for c in range(FG + Z0, FA, ZW)]
    fs.append(done(g.iota(T.win[:, FV:FG], [[0, FG - FV]], 0, 0, allow_small_or_imprecise_dtypes=True)))

    wait("g", [lw, lp])
    g.remote_dma_fused([
        RemoteDMATransfer(dst_ids=[dst(cores[q]) for q in grp], dma_engine_mask=bits(engs), remote_sem=T.sem.lin,
                          srcs=[T.lists[:, me, :]],
                          dsts=[T.lists[:, listener_order(q, cores, topo).index(rank), :] for q in grp])
        for grp, engs in ((far, far_eng), (near, near_eng))], local_sem=T.sem.sent)
    total["sent"] = len(far_eng) + len(near_eng)
    total["lin"] = len(far) * len(far_eng) + len(near) * len(near_eng)
    lin = ("lin", total["lin"])

    ident = T.cb[:, 136:264]
    nz = done(g.iota(T.nb[:], [[0, 136]], 0, 0, allow_small_or_imprecise_dtypes=True))
    pc = done(g.iota(T.pcol[:], [[0, 1]], 0, 1))
    wait("g", [nz, cz])
    n0 = done(g.affine_select(T.nb[:, 8:136], T.nb[:, 8:136], [[-16, 8], [1000, 2], [-1, 8]], OP.not_equal, -1.0, 0, 1))
    w0 = done(g.affine_select(T.cb[:, 8:136:16], T.cb[:, 8:136:16], [[-16, 8]], OP.is_ge, 0.5, -4, 1))
    w1 = done(g.affine_select(T.cb[:, 16:136:16], T.cb[:, 16:136:16], [[-16, 8]], OP.is_ge, -0.5, -4, 1))
    wait("g", [n0])
    nb_t = done(g.affine_select(T.nb[:, 8:136], T.nb[:, 8:136], [[-16, 8], [1000, 2], [-1, 8]], OP.not_equal, -1.0, -8, 1))
    wait("g", [w0, w1])
    w2 = done(g.affine_select(T.cb[:, 8:136:8], T.cb[:, 8:136:8], [[-16, 8], [0, 2]], OP.is_ge, 2.0 ** -13, -2, 1))
    id_t = done(g.affine_select(ident, ident, [[-1, 128]], OP.not_equal, 1.0, 0, 1))
    wait("g", [w2])
    wb_t = done(g.affine_select(T.cb[:, 8:136:8], T.cb[:, 8:136:8], [[-16, 8], [0, 2]], OP.is_ge, 0.0, 0, 1))

    pp = [b[:, 0:QC] for b in (T.pp0, T.pp1, T.pr2, T.pe2)]
    piece = lambda k, c: T.pcs[:, (4 * k + c) * QC:(4 * k + c + 1) * QC]
    bias = (786432.0, -2047.5, 0.0)
    rem, made = {}, {}
    wait("y", [fv] + fs)
    for _, k, c in sorted((k + LAG[c], k, c) for k in range(4) for c in range(4)):
        if k == 0:
            wait("v", [trk_t[c // 2]])
            rem[c] = done(V.tensor_copy(pp[c], T.trk[:, c * QC:(c + 1) * QC]))
        else:
            wait("v", [made[(k - 1, c)]])
            rem[c] = done(V.tensor_tensor(pp[c] if k < 3 else piece(3, c), pp[c], piece(k - 1, c), OP.subtract))
        if k < 3:
            wait("s", [rem[c]])
            made[(k, c)] = done(S.activation(piece(k, c), pp[c], AF.Identity, bias=bias[k]))
        else:
            made[(k, c)] = rem[c]
        if c % 2 == 1:
            h = c // 2
            wait("y", [made[(k, c - 1)], made[(k, c)]])
            win_t = done(Y.dma_start(T.win[k:128:16, h * H:(h + 1) * H], T.pcs[:, (2 * k + h) * HC:(2 * k + h + 1) * HC]), laid, 16)
    snd_t = done(Y.dma_start(T.snd[:], T.sound[:]), n=16)
    banks_free = [made[(3, c)] for c in range(4)]

    tw, pl = T.lists[:, :, 0:16], T.lists[:, :, 16:32]
    n_lo, n_hi = T.nb[:, 8:136], T.nb[:, 0:128]
    wait("v", [pc])
    h8 = done(V.tensor_scalar(T.h8[:], T.pcol[:], 8, None, OP.bitwise_and))
    wait("v", [h8])
    m0 = done(V.tensor_scalar(T.cols[:, 0:1], T.h8[:], 1.0 / 8, -1.0, OP.mult, OP.add))
    m1 = done(V.tensor_scalar(T.cols[:, 1:2], T.h8[:], -1.0 / 8, None, OP.mult))
    sg = done(V.tensor_scalar(T.cols[:, 3:4], T.h8[:], -0.25, 1.0, OP.mult, OP.add))
    bu = done(V.tensor_scalar(T.cols[:, 2:3], T.h8[:], 256.0, -2048.0, OP.mult, OP.add))
    wait("s", [nb_t, m0, m1])
    sh = [done(S.activation(T.sh[:, h, :], T.nb[:], AF.Identity, scale=T.cols[:, h:h + 1])) for h in range(2)]
    wait("s", [sg])
    rt = done(S.activation(T.rt[:], n_hi, AF.Identity, scale=T.cols[:, 3:4]))
    wait("v", [lin, lw, lp])
    xi = done(V.tensor_scalar(T.xy[:, 0:96], pl, 12, None, OP.arith_shift_right))
    yi = done(V.tensor_scalar(T.xy[:, 96:192], pl, 4095, None, OP.bitwise_and))
    o0 = done(V.tensor_copy(T.off[:], tw))
    th = done(V.tensor_copy(T.tt[:, 0:96], tw))
    wait("v", [xi, yi])
    xf = done(V.tensor_scalar(T.xf[:], T.xy[:], -2048.0, 0.5, OP.add, OP.mult))
    wait("v", [th])
    tl = done(V.tensor_tensor(T.tt[:, 96:192], tw, T.tt[:, 0:96], OP.subtract))
    wait("v", [nb_t, rt])
    rot = done(V.tensor_tensor(T.rot[:], n_lo, T.rt[:], OP.add))
    wait("t", sh + [xf] + banks_free)
    for h in range(2):
        for c in range(2):
            ins = PE.matmul(T.pp0[:, h:192:2], T.sh[:, h, 8 - 8 * c:136 - 8 * c], T.xf[:, 96 * c:96 * c + 96], h + c == 0, h + c == 2)
    xp = done(ins)
    wait("v", [xp])
    xd = done(V.tensor_copy(T.xd[:], T.pp0[:, 0:192]))

    NS = 3 * ROUNDS
    names = {(w, k): fresh() for w in ("ga", "p1", "ab", "p2", "cp") for k in range(3)}
    ga, p1, ab, p2, cp, cp1 = {}, {}, {}, {}, {}, {}
    R = lambda s: T["pr%d" % (s % 3)][:, 0:64]
    E = lambda s: T["pe%d" % (s % 3)][:, 0:32]

    def times(s):
        k = s % 3
        wait("t", [id_t, th, tl])
        for c in range(2):
            PE.matmul(E(s), ident, T.tt[:, 96 * c + 32 * k:96 * c + 32 * k + 32], c == 0, False)

    def gather(s):
        k = s % 3
        deps = [win_t, o0] if s < 3 else [cp[s - 3]]
        wait("s", deps)
        done(S.activation(T.gat[:, 512 * k:512 * k + 16 * CA], T.win[:, 0:L].indirect(T.off[:, 32 * k:32 * k + CA]), AF.Copy), names[("ga", k)])
        wait("v", deps)
        ga[s] = done(V.tensor_copy(T.gat[:, 512 * k + 16 * CA:512 * k + 512], T.win[:, 0:L].indirect(T.off[:, 32 * k + CA:32 * k + 32])), names[("ga", k)])

    def forms(s):
        k = s % 3
        wait("t", [rot, xd])
        PE.matmul(R(s), T.rot[:], T.xd[:, 64 * k:64 * k + 64], True, False)
        if s > 0:
            times(s - 1)
        wait("t", [wb_t, ga[s]])
        for a in range(8):
            ins = PE.matmul(R(s), T.cb[:, 8 - a:136 - a], T.gat[:, 512 * k + a:512 * k + 512:8], False, a == 7)
        p1[s] = done(ins, names[("p1", k)])

    def absolute(s):
        k = s % 3
        wait("s", [p1[s], bu])
        ab[s] = done(S.activation(T.ab[:, 64 * k:64 * k + 64], R(s), AF.Abs, bias=T.cols[:, 2:3]), names[("ab", k)])

    def emission(s):
        k = s % 3
        wait("t", [ab[s]])
        PE.matmul(E(s), n_lo, T.ab[:, 64 * k:64 * k + 64:2], False, False)
        p2[s] = done(PE.matmul(E(s), n_hi, T.ab[:, 64 * k + 1:64 * k + 64:2], False, True), names[("p2", k)])

    def offsets(s):
        k = s % 3
        wait("v", [p2[s]])
        cp[s] = done(V.tensor_copy(T.off[:, 32 * k:32 * k + 32], E(s)), names[("cp", k)])
        if s >= NS - 3:
            cp1[k] = done(V.tensor_scalar(T.off1[:, 32 * k:32 * k + 32], E(s), 1.0, None, OP.add))

    for s in range(NS):
        gather(s)
        if s >= 2:
            offsets(s - 2)
        if s >= 1:
            absolute(s - 1)
        forms(s)
        if s >= 1:
            emission(s - 1)

    first, u = {}, {}

    def sound_a(i, q="s", c0=0, c1=16):
        wait(q, [snd_t, cp[NS - 3 + i // 2]])
        out, src = T.s0[:, K * i + 16 * c0:K * i + 16 * c1], T.snd[:, 0:L].indirect(T.off[:, 16 * i + c0:16 * i + c1])
        first.setdefault(i, []).append(done(S.activation(out, src, AF.Copy) if q == "s" else V.tensor_copy(out, src)))

    def sound_b(i):
        wait("v", [snd_t, cp1[i // 2]] + first[i])
        out = T.land[:, rank, :] if i == me else T.ub[:, i, :]
        u[i] = done(V.tensor_tensor(out, T.snd[:, 0:L].indirect(T.off1[:, 16 * i:16 * i + 16]), T.s0[:, K * i:K * (i + 1)], OP.add))
        if i != me:
            q = order[i]
            engs = tile_engines(rank, q)
            rid, pid, _ = topo.addr(cores[q])
            wait("g", [u[i]])
            g.remote_dma(T.land[:, rank, :], T.ub[:, i, :], T.sem["arr%d" % rank], T.sem.sent, pid, rid, bits(engs))
            total["sent"] += len(engs)

    times(NS - 1)
    sound_a(0, "s", 0, 8)
    sound_a(0, "v", 8, 16)
    absolute(NS - 1)
    emission(NS - 1)
    sound_a(1)
    sound_b(0)
    offsets(NS - 2)
    sound_a(2)
    sound_b(1)
    offsets(NS - 1)
    for i in range(2, N):
        if i + 1 < N:
            sound_a(i + 1)
        sound_b(i)

    late = [q for q in near if listener_order(q, cores, topo)[me - 1] == rank][0]
    cut = min(late, rank)
    parts = ((T.pp0, 0, YA), (T.pp1, YA, K))
    ends = {}
    wait("t", [xd])
    for q, p in [(q, p) for q in range(cut) for p in range(2)] + [(q, p) for p in range(2) for q in range(cut, N)]:
        if q == rank:
            wait("t", [u[me]])
        else:
            total["arr%d" % q] = len(tile_engines(q, rank))
            wait("t", [("arr%d" % q, total["arr%d" % q])])
        bank, c0, c1 = parts[p]
        ends[p] = PE.matmul(bank[:, 0:c1 - c0], ident, T.land[:, q, c0:c1], q == 0, q == N - 1)
    sa, sb = done(ends[0]), done(ends[1])
    wait("s", [sa])
    ya = done(S.activation(T.ya[:], T.pp0[:, 0:YA], AF.Copy))
    wait("v", [sb])
    yb = done(V.tensor_copy(T.yb[:], T.pp1[:, 0:K - YA]))
    wait("s", [ya])
    done(S.dma_start(T.y[:, 0:YA], T.ya[:]), n=16)
    wait("y", [yb])
    done(Y.dma_start(T.y[:, YA:K], T.yb[:]), n=16)
    wait("g", [(n, v) for n, v in total.items() if best.get(n, 0) < v])
